import numpy as np
import ml_dtypes


def mxq(x, axis, fmt="e4m3"):
    dtype, down = {"e4m3": (ml_dtypes.float8_e4m3fn, 7), "e5m2": (ml_dtypes.float8_e5m2, 14)}[fmt]
    v = np.moveaxis(np.asarray(x, np.float32).astype(ml_dtypes.bfloat16).astype(np.float64), axis, -1)
    blocks = v.reshape(v.shape[:-1] + (-1, 32))
    amax = np.abs(blocks).max(-1, keepdims=True)
    byte = np.maximum(np.where(amax > 0, np.frexp(amax)[1] - 1 + 127, 0) - down, 1)
    scale = np.exp2(byte - 127.0)
    codes = (blocks / scale).astype(np.float32).astype(dtype).astype(np.float64)
    return np.moveaxis((codes * scale).reshape(v.shape), -1, axis)


WIDE = False


def mx_kscale(k):
    if not WIDE:
        return np.ones(k)
    levels = np.array([10, -10, 5, -5, 0])
    if k % 512:
        return np.exp2(np.random.permutation(np.resize(levels, k // 32))).repeat(32)
    a = np.empty((k // 512, 16))
    for p in range(k // 512):
        a[p, :8] = np.random.permutation(np.resize(levels, 8))
        for g in range(8):
            far = levels[np.abs(levels - a[p, g]) >= 10]
            a[p, g + 8] = far[np.random.randint(len(far))]
    return np.exp2(a.ravel()).repeat(32)


def f64(x):
    return np.asarray(x).astype(np.float64)


def striped(idx):
    return np.tile(idx.reshape(-1, 16).T, (8, 1)).astype(np.uint16)


def unstriped(offs):
    return offs[:16].T.reshape(-1).astype(np.int64)


def striped8(idx):
    return np.concatenate([x.reshape(-1, 16).T for x in idx]).astype(np.uint16)


def runs(offs, k):
    lists = np.stack([offs[16 * r : 16 * r + 16].T.reshape(-1) for r in range(8)]).astype(np.int64)
    return lists[np.arange(k) % 512 // 64]


def pack_weight(w):
    k, n = w.shape
    w = f64(np.asarray(w, np.float32).astype(ml_dtypes.bfloat16)).reshape(k // 32, 32, n)
    amax = np.abs(w).max(1)
    byte = np.clip(np.where(amax > 0, np.frexp(amax)[1] - 1 + 127 - 7, 1), 1, 254)
    scaled = (w * np.exp2(127.0 - byte)[:, None, :]).reshape(k, n).astype(np.float32)
    words = np.ascontiguousarray(scaled.reshape(k // 512, 128, 4, n).transpose(0, 1, 3, 2)).astype(ml_dtypes.float8_e4m3fn).view(np.uint8)
    return words, np.ascontiguousarray(byte.astype(np.uint8).reshape(k // 512, 16, n))


def unpack_weight(words, scales):
    g, p, n, _ = words.shape
    vals = np.ascontiguousarray(words).view(ml_dtypes.float8_e4m3fn).astype(np.float64) * np.repeat(np.exp2(scales.astype(np.float64) - 127.0), 8, axis=1)[..., None]
    return vals.transpose(0, 1, 3, 2).reshape(g * 512, n)


K, T, S, N, H = 512, 2048, 512, 512, 512


def setup_inputs():
    n = np.random.standard_normal
    s = mx_kscale(K)[:, None]
    u = mx_kscale(H)
    packed_xT = pack_weight(n((K, T)) * s)
    return {
        "x_words": packed_xT[0],
        "x_scales": packed_xT[1],
        "w1": (n((K, H)) / np.sqrt(K) / s).astype(np.float32),
        "gn": (np.random.uniform(0.5, 1.5, (H, 1)) * u[:, None]).astype(np.float32),
        "w2": (n((H, N)) / np.sqrt(H) / u[:, None]).astype(np.float32),
        "offs": striped(np.random.permutation(T)[:S]),
        "n1": striped8(np.stack([np.random.permutation(S) for _ in range(8)])),
        "n2": striped8(np.stack([np.random.permutation(S) for _ in range(8)])),
        "n3": striped8(np.stack([np.random.permutation(S) for _ in range(8)])),
        "n4": striped8(np.stack([np.random.permutation(S) for _ in range(8)])),
    }


def reference(x_words, x_scales, w1, gn, w2, offs, n1, n2, n3, n4):
    xq = unpack_weight(x_words, x_scales)[:, unstriped(offs)]
    y = mxq(f64(w1), 0, "e4m3").T @ xq
    ex = np.exp(0.5 * y)
    z = f64(gn) * ((ex * (y[np.arange(H)[:, None], runs(n1, H)])) / (ex + ex[np.arange(H)[:, None], runs(n2, H)]))
    h = mxq(f64(w2), 0, "e4m3").T @ mxq(z, 0, "e4m3")
    return np.maximum(h - (h[np.arange(N)[:, None], runs(n3, N)]), 0.5 * (h[np.arange(N)[:, None], runs(n4, N)]))

@@ -1,0 +1,201 @@
+from contextlib import ExitStack
+
+import concourse.mybir as mybir
+
+K, T, S, N, H = 512, 2048, 512, 512, 512
+FLOPS = 2 * K * H * S + 2 * H * N * S
+
+F32 = mybir.dt.float32
+BF16 = mybir.dt.bfloat16
+I32 = mybir.dt.int32
+U32 = mybir.dt.uint32
+U16 = mybir.dt.uint16
+U8 = mybir.dt.uint8
+FP8X4 = mybir.dt.float8_e4m3fn_x4
+ALU = mybir.AluOpType
+ACT = mybir.ActivationFunctionType
+
+P = 128
+PACK = 4
+HALF = S // 2
+VECTOR_COLS = 160
+
+
+def tile_picked_sharelay_none_p_kernel(tc, x_words, x_scales, w1, gn, w2, offs, n1, n2, n3, n4, out):
+    nc = tc.nc
+    cols = [slice(h * HALF, (h + 1) * HALF) for h in range(2)]
+    entries = [slice(h * HALF // 16, (h + 1) * HALF // 16) for h in range(2)]
+
+    with ExitStack() as ctx:
+        keep = ctx.enter_context(tc.tile_pool(name="keep", bufs=1))
+        psum = ctx.enter_context(tc.psum_pool(name="psum", bufs=1))
+
+        def sbuf(name, shape, dtype, tag=None):
+            return keep.tile(shape, dtype, name=name, tag=tag or name, align_bytes=64)
+
+        def load_list(name, source):
+            tile = keep.tile([P, S // 16], U16, name=name)
+            nc.sync.dma_start(tile[:], source)
+            return tile
+
+        def load_weight(name, source):
+            tile = sbuf(name, [P, PACK, 512], F32)
+            nc.sync.dma_start(out=tile[:], in_=source.rearrange("(p j) c -> p j c", j=PACK))
+            return tile
+
+        def deal(copy, raw, u, grouped):
+            copy(
+                out=grouped[:].rearrange("p (e m j) -> p m j e", e=2, j=PACK),
+                in_=raw[:].rearrange("p j (m u e) -> p u m j e", u=2, e=2)[:, u],
+            )
+
+        def quantize(name, grouped):
+            codes = sbuf(name + "_codes", [P, 2 * P], U32)
+            scales = sbuf(name + "_scales", [P, 2 * P], U8)
+            nc.vector.quantize_mx(out=codes[:].bitcast(FP8X4), scales=scales[:], in_=grouped[:])
+            return codes, scales
+
+        def product(bank, weights, t, codes, scales, where):
+            w_codes, w_scales = weights[t // 2]
+            m = slice(t % 2 * P, (t % 2 + 1) * P)
+            nc.tensor.matmul_mx(
+                out=bank, lhsT=w_codes[:, m].bitcast(FP8X4), lhsT_scale=w_scales[:, m],
+                rhs=codes[:, where].bitcast(FP8X4), rhs_scale=scales[:, where], start=True, stop=True,
+            )
+
+        x_scale_table = sbuf("x_scale_table", [P, T], U8)
+        nc.gpsimd.memset(x_scale_table[:].bitcast(I32), 0)
+        warm = sbuf("warm", [P, 1], F32)
+        warm_out = sbuf("warm_out", [P, 1], F32)
+        nc.vector.memset(warm[:], 0.0)
+        for q in range(4):
+            nc.gpsimd.dma_start(
+                out=x_scale_table[32 * q : 32 * q + 4, :].bitcast(I32),
+                in_=x_scales[0, 4 * q : 4 * q + 4, :].bitcast(I32),
+            )
+        nc.scalar.activation(out=warm_out[:], in_=warm[:], func=ACT.Sigmoid, scale=-0.5)
+
+        offs_sb = load_list("offs_sb", offs)
+        w1_raw = load_weight("w1_raw", w1)
+        x_word_table = sbuf("x_word_table", [P, T], U32)
+        nc.sync.dma_start(
+            out=x_word_table[:].bitcast(I32),
+            in_=x_words[0].rearrange("p n t -> p (n t)").bitcast(I32),
+        )
+        n2_sb = load_list("n2_sb", n2)
+        gn_sb = sbuf("gn_sb", [P, PACK], F32)
+        nc.sync.dma_start(out=gn_sb[:], in_=gn.rearrange("(p t) o -> p (t o)", t=PACK))
+        n1_sb = load_list("n1_sb", n1)
+        w2_raw = load_weight("w2_raw", w2)
+        n4_sb = load_list("n4_sb", n4)
+        n3_sb = load_list("n3_sb", n3)
+
+        x_sc = sbuf("x_sc", [P, S], U8)
+        nc.vector.tensor_copy(x_sc[:], x_scale_table[:].indirect(offs_sb[:]))
+        w1_grouped = [sbuf("w1_grouped%d" % u, [P, 2 * P * PACK], BF16) for u in range(2)]
+        deal(nc.vector.tensor_copy, w1_raw, 0, w1_grouped[0])
+        deal(nc.scalar.copy, w1_raw, 1, w1_grouped[1])
+        w1_mx = [quantize("w1_%d" % u, w1_grouped[u]) for u in range(2)]
+        x_codes = sbuf("x_codes", [P, S], U32)
+        for h in range(2):
+            nc.vector.tensor_copy(x_codes[:, cols[h]], x_word_table[:].indirect(offs_sb[:, entries[h]]))
+
+        def products(stage, weights, codes, scales):
+            first = [psum.tile([P, HALF], F32, name="%s_half%d" % (stage, h), tag="half%d" % h) for h in range(2)]
+            for h in range(2):
+                product(first[h][:], weights, 0, codes, scales, cols[h])
+            rest = {}
+            for t in range(1, PACK):
+                rest[t] = psum.tile([P, S], F32, name="%s_bank%d" % (stage, t), tag="bank%d" % t)
+                product(rest[t][:], weights, t, codes, scales, slice(0, S))
+            return first, rest
+
+        y_first, y_rest = products("y", w1_mx, x_codes, x_sc)
+
+        y_win = [sbuf("y_win%d" % t, [P, S], F32) for t in range(PACK)]
+        y_plain = [sbuf("y_plain%d" % t, [P, S], F32) for t in range(PACK)]
+        gy_win = [sbuf("gy_win%d" % t, [P, S], F32) for t in range(PACK)]
+        diff = [sbuf("diff%d" % t, [P, S], F32) for t in range(PACK)]
+        share = [sbuf("share%d" % t, [P, S], F32) for t in range(PACK)]
+        z = [sbuf("z%d" % h, [P, PACK, HALF], F32) for h in range(2)]
+
+        def sigmoid(t, h):
+            nc.scalar.activation(out=share[t][:, cols[h]], in_=diff[t][:, cols[h]], func=ACT.Sigmoid, scale=-0.5)
+
+        def make_z(t, h):
+            nc.vector.tensor_tensor(z[h][:, t, :], gy_win[t][:].indirect(n1_sb[:, entries[h]]), share[t][:, cols[h]], ALU.mult)
+
+        for t in range(PACK):
+            if t == 0:
+                for h in range(2):
+                    nc.scalar.copy(out=y_win[0][:, cols[h]], in_=y_first[h][:])
+                    nc.scalar.copy(out=y_plain[0][:, cols[h]], in_=y_first[h][:])
+            else:
+                nc.scalar.copy(out=y_win[t][:], in_=y_rest[t][:])
+                nc.scalar.copy(out=y_plain[t][:], in_=y_rest[t][:])
+            for h in range(2):
+                nc.vector.tensor_tensor(diff[t][:, cols[h]], y_win[t][:].indirect(n2_sb[:, entries[h]]), y_plain[t][:, cols[h]], ALU.subtract)
+            if t < 2:
+                nc.vector.tensor_scalar(gy_win[t][:], y_plain[t][:], gn_sb[:, t : t + 1], None, ALU.mult)
+            if t > 0:
+                if t - 1 >= 2:
+                    nc.scalar.activation(out=gy_win[t - 1][:], in_=y_rest[t - 1][:], func=ACT.Copy, scale=gn_sb[:, t - 1 : t])
+                sigmoid(t - 1, 0)
+                make_z(t - 1, 0)
+        nc.scalar.activation(out=gy_win[3][:], in_=y_rest[3][:], func=ACT.Copy, scale=gn_sb[:, 3:4])
+        sigmoid(PACK - 1, 0)
+        make_z(PACK - 1, 0)
+        for t in range(PACK):
+            sigmoid(t, 1)
+            make_z(t, 1)
+
+        w2_grouped0 = sbuf("w2_grouped0", [P, 2 * P * PACK], BF16)
+        deal(nc.scalar.copy, w2_raw, 0, w2_grouped0)
+
+        z_grouped = [sbuf("z_grouped%d" % h, [P, HALF * PACK], BF16) for h in range(2)]
+
+        def weave(copy, h, c0, c1):
+            copy(
+                out=z_grouped[h][:, c0 * PACK : c1 * PACK].rearrange("p (c i t) -> p c t i", i=4, t=PACK),
+                in_=z[h][:, :, c0:c1].rearrange("p t (c i) -> p c t i", i=4),
+            )
+
+        weave(nc.scalar.copy, 0, 0, HALF)
+        weave(nc.vector.tensor_copy, 1, 0, VECTOR_COLS)
+        weave(nc.scalar.copy, 1, VECTOR_COLS, HALF)
+        w2_mx = [quantize("w2_0", w2_grouped0)]
+        z_codes = sbuf("z_codes", [P, S], U32)
+        z_scales = sbuf("z_scales", [P, S], U8)
+        for h in range(2):
+            nc.vector.quantize_mx(out=z_codes[:, cols[h]].bitcast(FP8X4), scales=z_scales[:, cols[h]], in_=z_grouped[h][:])
+        w2_grouped1 = sbuf("w2_grouped1", [P, 2 * P * PACK], BF16, tag="z_grouped1")
+        deal(nc.vector.tensor_copy, w2_raw, 1, w2_grouped1)
+        w2_mx.append(quantize("w2_1", w2_grouped1))
+
+        h_first, h_rest = products("h", w2_mx, z_codes, z_scales)
+
+        out_rows = out.rearrange("(p t) n -> p t n", t=PACK)
+        for t in range(PACK):
+            neg_win = sbuf("neg_win%d" % t, [P, S], F32)
+            h_plain = sbuf("h_plain%d" % t, [P, S], F32)
+            if t == 0:
+                for h in range(2):
+                    nc.scalar.activation(out=neg_win[:, cols[h]], in_=h_first[h][:], func=ACT.Copy, scale=-1.0)
+                for h in range(2):
+                    nc.scalar.copy(out=h_plain[:, cols[h]], in_=h_first[h][:])
+            else:
+                nc.scalar.activation(out=neg_win[:], in_=h_rest[t][:], func=ACT.Copy, scale=-1.0)
+                nc.scalar.copy(out=h_plain[:], in_=h_rest[t][:])
+            neg4 = sbuf("neg4_%d" % t, [P, S], F32)
+            gap = sbuf("gap%d" % t, [P, S], F32)
+            result = sbuf("result%d" % t, [P, S], F32)
+            for h in range(2):
+                nc.vector.tensor_copy(neg4[:, cols[h]], neg_win[:].indirect(n4_sb[:, entries[h]]))
+            for h in range(2):
+                nc.vector.tensor_tensor(gap[:, cols[h]], neg_win[:].indirect(n3_sb[:, entries[h]]), h_plain[:, cols[h]], ALU.add)
+            for h in range(2):
+                nc.vector.scalar_tensor_tensor(result[:, cols[h]], neg4[:, cols[h]], -0.5, gap[:, cols[h]], ALU.mult, ALU.max)
+                if t == PACK - 1:
+                    nc.sync.dma_start(out=out_rows[:, t, cols[h]], in_=result[:, cols[h]])
+            if t < PACK - 1:
+                nc.sync.dma_start(out=out_rows[:, t, :], in_=result[:])

@@ -39,7 +39,7 @@ def tile_picked_sharelay_none_p_kernel(tc, x_words, x_scales, w1, gn, w2, offs, 
             return tile
 
         def load_weight(name, source):
-            tile = sbuf(name, [P, PACK, 512], F32)
+            tile = sbuf(name, [P, PACK, 512], F32, tag="raw_weight")
             nc.sync.dma_start(out=tile[:], in_=source.rearrange("(p j) c -> p j c", j=PACK))
             return tile
 
@@ -64,29 +64,28 @@ def tile_picked_sharelay_none_p_kernel(tc, x_words, x_scales, w1, gn, w2, offs, 
             )
 
         x_scale_table = sbuf("x_scale_table", [P, T], U8)
-        nc.gpsimd.memset(x_scale_table[:].bitcast(I32), 0)
+        nc.vector.memset(x_scale_table[:].bitcast(I32), 0)
         warm = sbuf("warm", [P, 1], F32)
         warm_out = sbuf("warm_out", [P, 1], F32)
         nc.vector.memset(warm[:], 0.0)
         for q in range(4):
-            nc.gpsimd.dma_start(
+            nc.scalar.dma_start(
                 out=x_scale_table[32 * q : 32 * q + 4, :].bitcast(I32),
                 in_=x_scales[0, 4 * q : 4 * q + 4, :].bitcast(I32),
             )
         nc.scalar.activation(out=warm_out[:], in_=warm[:], func=ACT.Sigmoid, scale=-0.5)
 
         offs_sb = load_list("offs_sb", offs)
+        n2_sb = load_list("n2_sb", n2)
+        n1_sb = load_list("n1_sb", n1)
         w1_raw = load_weight("w1_raw", w1)
         x_word_table = sbuf("x_word_table", [P, T], U32)
         nc.sync.dma_start(
             out=x_word_table[:].bitcast(I32),
             in_=x_words[0].rearrange("p n t -> p (n t)").bitcast(I32),
         )
-        n2_sb = load_list("n2_sb", n2)
-        gn_sb = sbuf("gn_sb", [P, PACK], F32)
+        gn_sb = sbuf("gn_sb", [P, PACK], F32, tag="warm")
         nc.sync.dma_start(out=gn_sb[:], in_=gn.rearrange("(p t) o -> p (t o)", t=PACK))
-        n1_sb = load_list("n1_sb", n1)
-        w2_raw = load_weight("w2_raw", w2)
         n4_sb = load_list("n4_sb", n4)
         n3_sb = load_list("n3_sb", n3)
 
@@ -95,6 +94,7 @@ def tile_picked_sharelay_none_p_kernel(tc, x_words, x_scales, w1, gn, w2, offs, 
         w1_grouped = [sbuf("w1_grouped%d" % u, [P, 2 * P * PACK], BF16) for u in range(2)]
         deal(nc.vector.tensor_copy, w1_raw, 0, w1_grouped[0])
         deal(nc.scalar.copy, w1_raw, 1, w1_grouped[1])
+        w2_raw = load_weight("w2_raw", w2)
         w1_mx = [quantize("w1_%d" % u, w1_grouped[u]) for u in range(2)]
         x_codes = sbuf("x_codes", [P, S], U32)
         for h in range(2):
@@ -112,11 +112,15 @@ def tile_picked_sharelay_none_p_kernel(tc, x_words, x_scales, w1, gn, w2, offs, 
 
         y_first, y_rest = products("y", w1_mx, x_codes, x_sc)
 
-        y_win = [sbuf("y_win%d" % t, [P, S], F32) for t in range(PACK)]
-        y_plain = [sbuf("y_plain%d" % t, [P, S], F32) for t in range(PACK)]
+        y_win = [sbuf("y_win%d" % t, [P, S if t == 0 else 2 * S], F32) for t in range(PACK)]
+        y_last = sbuf("y_last", [P, S], F32)
+        y_plain = [y_win[t + 1][:, S:] for t in range(PACK - 1)] + [y_last[:]]
+        neg_win = [sbuf("neg_win%d" % t, [P, 2 * S], F32) for t in range(PACK)]
+        h_last = sbuf("h_last", [P, S], F32)
+        h_plain = [neg_win[t + 1][:, S:] for t in range(PACK - 1)] + [h_last[:]]
         gy_win = [sbuf("gy_win%d" % t, [P, S], F32) for t in range(PACK)]
         diff = [sbuf("diff%d" % t, [P, S], F32) for t in range(PACK)]
-        share = [sbuf("share%d" % t, [P, S], F32) for t in range(PACK)]
+        share = [sbuf("share%d" % t, [P, S], F32)[:] for t in range(PACK - 1)] + [neg_win[0][:, S:]]
         z = [sbuf("z%d" % h, [P, PACK, HALF], F32) for h in range(2)]
 
         def sigmoid(t, h):
@@ -131,12 +135,15 @@ def tile_picked_sharelay_none_p_kernel(tc, x_words, x_scales, w1, gn, w2, offs, 
                     nc.scalar.copy(out=y_win[0][:, cols[h]], in_=y_first[h][:])
                     nc.scalar.copy(out=y_plain[0][:, cols[h]], in_=y_first[h][:])
             else:
-                nc.scalar.copy(out=y_win[t][:], in_=y_rest[t][:])
-                nc.scalar.copy(out=y_plain[t][:], in_=y_rest[t][:])
-            for h in range(2):
-                nc.vector.tensor_tensor(diff[t][:, cols[h]], y_win[t][:].indirect(n2_sb[:, entries[h]]), y_plain[t][:, cols[h]], ALU.subtract)
+                nc.scalar.copy(out=y_win[t][:, :S], in_=y_rest[t][:])
+                nc.scalar.copy(out=y_plain[t], in_=y_rest[t][:])
+            if t == 0:
+                for h in range(2):
+                    nc.vector.tensor_tensor(diff[t][:, cols[h]], y_win[t][:].indirect(n2_sb[:, entries[h]]), y_plain[t][:, cols[h]], ALU.subtract)
+            else:
+                nc.vector.tensor_tensor(diff[t][:], y_win[t][:].indirect(n2_sb[:]), y_plain[t], ALU.subtract)
             if t < 2:
-                nc.vector.tensor_scalar(gy_win[t][:], y_plain[t][:], gn_sb[:, t : t + 1], None, ALU.mult)
+                nc.vector.tensor_scalar(gy_win[t][:], y_plain[t], gn_sb[:, t : t + 1], None, ALU.mult)
             if t > 0:
                 if t - 1 >= 2:
                     nc.scalar.activation(out=gy_win[t - 1][:], in_=y_rest[t - 1][:], func=ACT.Copy, scale=gn_sb[:, t - 1 : t])
@@ -175,27 +182,30 @@ def tile_picked_sharelay_none_p_kernel(tc, x_words, x_scales, w1, gn, w2, offs, 
         h_first, h_rest = products("h", w2_mx, z_codes, z_scales)
 
         out_rows = out.rearrange("(p t) n -> p t n", t=PACK)
+        neg4 = [sbuf("neg4_%d" % t, [P, S], F32) for t in range(PACK)]
+        gap = [sbuf("gap%d" % t, [P, S], F32) for t in range(PACK)]
+        result = [sbuf("result%d" % t, [P, S], F32) for t in range(PACK)]
+
+        def finish(t, where):
+            nc.vector.scalar_tensor_tensor(result[t][:, where], neg4[t][:, where], -0.5, gap[t][:, where], ALU.mult, ALU.max)
+            nc.sync.dma_start(out=out_rows[:, t, where], in_=result[t][:, where])
+
         for t in range(PACK):
-            neg_win = sbuf("neg_win%d" % t, [P, S], F32)
-            h_plain = sbuf("h_plain%d" % t, [P, S], F32)
             if t == 0:
                 for h in range(2):
-                    nc.scalar.activation(out=neg_win[:, cols[h]], in_=h_first[h][:], func=ACT.Copy, scale=-1.0)
+                    nc.scalar.activation(out=neg_win[0][:, cols[h]], in_=h_first[h][:], func=ACT.Copy, scale=-1.0)
                 for h in range(2):
-                    nc.scalar.copy(out=h_plain[:, cols[h]], in_=h_first[h][:])
+                    nc.scalar.copy(out=h_plain[0][:, cols[h]], in_=h_first[h][:])
             else:
-                nc.scalar.activation(out=neg_win[:], in_=h_rest[t][:], func=ACT.Copy, scale=-1.0)
-                nc.scalar.copy(out=h_plain[:], in_=h_rest[t][:])
-            neg4 = sbuf("neg4_%d" % t, [P, S], F32)
-            gap = sbuf("gap%d" % t, [P, S], F32)
-            result = sbuf("result%d" % t, [P, S], F32)
-            for h in range(2):
-                nc.vector.tensor_copy(neg4[:, cols[h]], neg_win[:].indirect(n4_sb[:, entries[h]]))
-            for h in range(2):
-                nc.vector.tensor_tensor(gap[:, cols[h]], neg_win[:].indirect(n3_sb[:, entries[h]]), h_plain[:, cols[h]], ALU.add)
-            for h in range(2):
-                nc.vector.scalar_tensor_tensor(result[:, cols[h]], neg4[:, cols[h]], -0.5, gap[:, cols[h]], ALU.mult, ALU.max)
-                if t == PACK - 1:
-                    nc.sync.dma_start(out=out_rows[:, t, cols[h]], in_=result[:, cols[h]])
+                nc.scalar.activation(out=neg_win[t][:, :S], in_=h_rest[t][:], func=ACT.Copy, scale=-1.0)
+                nc.scalar.copy(out=h_plain[t], in_=h_rest[t][:])
+            nc.vector.tensor_copy(neg4[t][:], neg_win[t][:].indirect(n4_sb[:]))
+            if t > 0:
+                finish(t - 1, slice(0, S))
             if t < PACK - 1:
-                nc.sync.dma_start(out=out_rows[:, t, :], in_=result[:])
+                nc.vector.tensor_tensor(gap[t][:], neg_win[t][:].indirect(n3_sb[:]), h_plain[t], ALU.add)
+            else:
+                for h in range(2):
+                    nc.vector.tensor_tensor(gap[t][:, cols[h]], neg_win[t][:].indirect(n3_sb[:, entries[h]]), h_plain[t][:, cols[h]], ALU.add)
+        for h in range(2):
+            finish(PACK - 1, cols[h])

@@ -19,6 +19,7 @@ P = 128
 PACK = 4
 HALF = S // 2
 VECTOR_COLS = 160
+LARGEST = 2.0 ** 126
 
 
 def tile_picked_sharelay_none_p_kernel(tc, x_words, x_scales, w1, gn, w2, offs, n1, n2, n3, n4, out):
@@ -49,15 +50,14 @@ def tile_picked_sharelay_none_p_kernel(tc, x_words, x_scales, w1, gn, w2, offs, 
                 in_=raw[:].rearrange("p j (m u e) -> p u m j e", u=2, e=2)[:, u],
             )
 
-        def quantize(name, grouped):
-            codes = sbuf(name + "_codes", [P, 2 * P], U32)
-            scales = sbuf(name + "_scales", [P, 2 * P], U8)
-            nc.vector.quantize_mx(out=codes[:].bitcast(FP8X4), scales=scales[:], in_=grouped[:])
-            return codes, scales
+        def quantize(weights, u, grouped):
+            codes, scales = weights
+            pair = slice(2 * u * P, 2 * (u + 1) * P)
+            nc.vector.quantize_mx(out=codes[:, pair].bitcast(FP8X4), scales=scales[:, pair], in_=grouped[:])
 
         def product(bank, weights, t, codes, scales, where):
-            w_codes, w_scales = weights[t // 2]
-            m = slice(t % 2 * P, (t % 2 + 1) * P)
+            w_codes, w_scales = weights
+            m = slice(t * P, (t + 1) * P)
             nc.tensor.matmul_mx(
                 out=bank, lhsT=w_codes[:, m].bitcast(FP8X4), lhsT_scale=w_scales[:, m],
                 rhs=codes[:, where].bitcast(FP8X4), rhs_scale=scales[:, where], start=True, stop=True,
@@ -69,36 +69,45 @@ def tile_picked_sharelay_none_p_kernel(tc, x_words, x_scales, w1, gn, w2, offs, 
         warm_out = sbuf("warm_out", [P, 1], F32)
         nc.vector.memset(warm[:], 0.0)
         for q in range(4):
-            nc.scalar.dma_start(
+            nc.sync.dma_start(
                 out=x_scale_table[32 * q : 32 * q + 4, :].bitcast(I32),
                 in_=x_scales[0, 4 * q : 4 * q + 4, :].bitcast(I32),
             )
         nc.scalar.activation(out=warm_out[:], in_=warm[:], func=ACT.Sigmoid, scale=-0.5)
 
         offs_sb = load_list("offs_sb", offs)
-        n2_sb = load_list("n2_sb", n2)
-        n1_sb = load_list("n1_sb", n1)
         w1_raw = load_weight("w1_raw", w1)
+        gn_sb = sbuf("gn_sb", [P, PACK], F32)
+        nc.sync.dma_start(out=gn_sb[:], in_=gn.rearrange("(p t) o -> p (t o)", t=PACK))
+        n2_sb = load_list("n2_sb", n2)
         x_word_table = sbuf("x_word_table", [P, T], U32)
         nc.sync.dma_start(
             out=x_word_table[:].bitcast(I32),
             in_=x_words[0].rearrange("p n t -> p (n t)").bitcast(I32),
         )
-        gn_sb = sbuf("gn_sb", [P, PACK], F32, tag="warm")
-        nc.sync.dma_start(out=gn_sb[:], in_=gn.rearrange("(p t) o -> p (t o)", t=PACK))
+        n1_sb = load_list("n1_sb", n1)
         n4_sb = load_list("n4_sb", n4)
         n3_sb = load_list("n3_sb", n3)
 
-        x_sc = sbuf("x_sc", [P, S], U8)
-        nc.vector.tensor_copy(x_sc[:], x_scale_table[:].indirect(offs_sb[:]))
         w1_grouped = [sbuf("w1_grouped%d" % u, [P, 2 * P * PACK], BF16) for u in range(2)]
         deal(nc.vector.tensor_copy, w1_raw, 0, w1_grouped[0])
         deal(nc.scalar.copy, w1_raw, 1, w1_grouped[1])
         w2_raw = load_weight("w2_raw", w2)
-        w1_mx = [quantize("w1_%d" % u, w1_grouped[u]) for u in range(2)]
+        slope = sbuf("slope", [P, PACK], F32)
+        bounded = sbuf("bounded", [P, PACK], F32)
+        inverse = sbuf("inverse", [P, PACK], F32)
+        nc.vector.reciprocal(inverse[:], gn_sb[:])
+        nc.gpsimd.tensor_scalar(bounded[:], inverse[:], LARGEST, -LARGEST, ALU.min, ALU.max)
+        nc.gpsimd.tensor_scalar(slope[:], bounded[:], -0.5, 0.0, ALU.mult, ALU.add)
+
+        x_sc = sbuf("x_sc", [P, S], U8)
+        nc.vector.tensor_copy(x_sc[:], x_scale_table[:].indirect(offs_sb[:]))
+        w1_mx = sbuf("w1_codes", [P, H], U32, tag="x_scale_table"), sbuf("w1_scales", [P, H], U8)
+        quantize(w1_mx, 0, w1_grouped[0])
         x_codes = sbuf("x_codes", [P, S], U32)
         for h in range(2):
             nc.vector.tensor_copy(x_codes[:, cols[h]], x_word_table[:].indirect(offs_sb[:, entries[h]]))
+        quantize(w1_mx, 1, w1_grouped[1])
 
         def products(stage, weights, codes, scales):
             first = [psum.tile([P, HALF], F32, name="%s_half%d" % (stage, h), tag="half%d" % h) for h in range(2)]
@@ -118,46 +127,41 @@ def tile_picked_sharelay_none_p_kernel(tc, x_words, x_scales, w1, gn, w2, offs, 
         neg_win = [sbuf("neg_win%d" % t, [P, 2 * S], F32) for t in range(PACK)]
         h_last = sbuf("h_last", [P, S], F32)
         h_plain = [neg_win[t + 1][:, S:] for t in range(PACK - 1)] + [h_last[:]]
-        gy_win = [sbuf("gy_win%d" % t, [P, S], F32) for t in range(PACK)]
         diff = [sbuf("diff%d" % t, [P, S], F32) for t in range(PACK)]
         share = [sbuf("share%d" % t, [P, S], F32)[:] for t in range(PACK - 1)] + [neg_win[0][:, S:]]
         z = [sbuf("z%d" % h, [P, PACK, HALF], F32) for h in range(2)]
 
         def sigmoid(t, h):
-            nc.scalar.activation(out=share[t][:, cols[h]], in_=diff[t][:, cols[h]], func=ACT.Sigmoid, scale=-0.5)
+            nc.scalar.activation(out=share[t][:, cols[h]], in_=diff[t][:, cols[h]], func=ACT.Sigmoid, scale=slope[:, t : t + 1])
 
         def make_z(t, h):
-            nc.vector.tensor_tensor(z[h][:, t, :], gy_win[t][:].indirect(n1_sb[:, entries[h]]), share[t][:, cols[h]], ALU.mult)
+            nc.vector.tensor_tensor(z[h][:, t, :], y_win[t][:].indirect(n1_sb[:, entries[h]]), share[t][:, cols[h]], ALU.mult)
+
+        def leave(dst, bank, t):
+            nc.scalar.activation(out=dst, in_=bank, func=ACT.Copy, scale=gn_sb[:, t : t + 1])
 
         for t in range(PACK):
             if t == 0:
                 for h in range(2):
-                    nc.scalar.copy(out=y_win[0][:, cols[h]], in_=y_first[h][:])
-                    nc.scalar.copy(out=y_plain[0][:, cols[h]], in_=y_first[h][:])
-            else:
-                nc.scalar.copy(out=y_win[t][:, :S], in_=y_rest[t][:])
-                nc.scalar.copy(out=y_plain[t], in_=y_rest[t][:])
-            if t == 0:
+                    leave(y_win[0][:, cols[h]], y_first[h][:], 0)
+                    leave(y_plain[0][:, cols[h]], y_first[h][:], 0)
                 for h in range(2):
                     nc.vector.tensor_tensor(diff[t][:, cols[h]], y_win[t][:].indirect(n2_sb[:, entries[h]]), y_plain[t][:, cols[h]], ALU.subtract)
             else:
+                leave(y_win[t][:, :S], y_rest[t][:], t)
+                leave(y_plain[t], y_rest[t][:], t)
                 nc.vector.tensor_tensor(diff[t][:], y_win[t][:].indirect(n2_sb[:]), y_plain[t], ALU.subtract)
-            if t < 2:
-                nc.vector.tensor_scalar(gy_win[t][:], y_plain[t], gn_sb[:, t : t + 1], None, ALU.mult)
-            if t > 0:
-                if t - 1 >= 2:
-                    nc.scalar.activation(out=gy_win[t - 1][:], in_=y_rest[t - 1][:], func=ACT.Copy, scale=gn_sb[:, t - 1 : t])
                 sigmoid(t - 1, 0)
                 make_z(t - 1, 0)
-        nc.scalar.activation(out=gy_win[3][:], in_=y_rest[3][:], func=ACT.Copy, scale=gn_sb[:, 3:4])
+        w2_grouped0 = sbuf("w2_grouped0", [P, 2 * P * PACK], BF16)
+        deal(nc.scalar.copy, w2_raw, 0, w2_grouped0)
+        w2_mx = sbuf("w2_codes", [P, N], U32), sbuf("w2_scales", [P, N], U8)
+        quantize(w2_mx, 0, w2_grouped0)
         sigmoid(PACK - 1, 0)
         make_z(PACK - 1, 0)
         for t in range(PACK):
             sigmoid(t, 1)
             make_z(t, 1)
-
-        w2_grouped0 = sbuf("w2_grouped0", [P, 2 * P * PACK], BF16)
-        deal(nc.scalar.copy, w2_raw, 0, w2_grouped0)
 
         z_grouped = [sbuf("z_grouped%d" % h, [P, HALF * PACK], BF16) for h in range(2)]
 
@@ -170,14 +174,13 @@ def tile_picked_sharelay_none_p_kernel(tc, x_words, x_scales, w1, gn, w2, offs, 
         weave(nc.scalar.copy, 0, 0, HALF)
         weave(nc.vector.tensor_copy, 1, 0, VECTOR_COLS)
         weave(nc.scalar.copy, 1, VECTOR_COLS, HALF)
-        w2_mx = [quantize("w2_0", w2_grouped0)]
         z_codes = sbuf("z_codes", [P, S], U32)
         z_scales = sbuf("z_scales", [P, S], U8)
         for h in range(2):
             nc.vector.quantize_mx(out=z_codes[:, cols[h]].bitcast(FP8X4), scales=z_scales[:, cols[h]], in_=z_grouped[h][:])
         w2_grouped1 = sbuf("w2_grouped1", [P, 2 * P * PACK], BF16, tag="z_grouped1")
         deal(nc.vector.tensor_copy, w2_raw, 1, w2_grouped1)
-        w2_mx.append(quantize("w2_1", w2_grouped1))
+        quantize(w2_mx, 1, w2_grouped1)
 
         h_first, h_rest = products("h", w2_mx, z_codes, z_scales)
 
@@ -187,7 +190,7 @@ def tile_picked_sharelay_none_p_kernel(tc, x_words, x_scales, w1, gn, w2, offs, 
         result = [sbuf("result%d" % t, [P, S], F32) for t in range(PACK)]
 
         def finish(t, where):
-            nc.vector.scalar_tensor_tensor(result[t][:, where], neg4[t][:, where], -0.5, gap[t][:, where], ALU.mult, ALU.max)
+            nc.vector.tensor_tensor(result[t][:, where], neg4[t][:, where], gap[t][:, where], ALU.max)
             nc.sync.dma_start(out=out_rows[:, t, where], in_=result[t][:, where])
 
         for t in range(PACK):
@@ -199,7 +202,7 @@ def tile_picked_sharelay_none_p_kernel(tc, x_words, x_scales, w1, gn, w2, offs, 
             else:
                 nc.scalar.activation(out=neg_win[t][:, :S], in_=h_rest[t][:], func=ACT.Copy, scale=-1.0)
                 nc.scalar.copy(out=h_plain[t], in_=h_rest[t][:])
-            nc.vector.tensor_copy(neg4[t][:], neg_win[t][:].indirect(n4_sb[:]))
+            nc.vector.tensor_scalar(neg4[t][:], neg_win[t][:].indirect(n4_sb[:]), -0.5, 0.0, ALU.mult, ALU.add)
             if t > 0:
                 finish(t - 1, slice(0, S))
             if t < PACK - 1:

@@ -18,7 +18,8 @@ ACT = mybir.ActivationFunctionType
 P = 128
 PACK = 4
 HALF = S // 2
-VECTOR_COLS = 160
+PAIR = 2 * P * PACK
+CHUNKS = ((0, 256), (256, 384), (384, 512))
 LARGEST = 2.0 ** 126
 
 
@@ -26,6 +27,9 @@ def tile_picked_sharelay_none_p_kernel(tc, x_words, x_scales, w1, gn, w2, offs, 
     nc = tc.nc
     cols = [slice(h * HALF, (h + 1) * HALF) for h in range(2)]
     entries = [slice(h * HALF // 16, (h + 1) * HALF // 16) for h in range(2)]
+
+    chunks = [slice(a, b) for a, b in CHUNKS]
+    chunk_entries = [slice(a // 16, b // 16) for a, b in CHUNKS]
 
     with ExitStack() as ctx:
         keep = ctx.enter_context(tc.tile_pool(name="keep", bufs=1))
@@ -44,16 +48,16 @@ def tile_picked_sharelay_none_p_kernel(tc, x_words, x_scales, w1, gn, w2, offs, 
             nc.sync.dma_start(out=tile[:], in_=source.rearrange("(p j) c -> p j c", j=PACK))
             return tile
 
-        def deal(copy, raw, u, grouped):
+        def deal(copy, raw, u, grouped, m=slice(0, P)):
             copy(
-                out=grouped[:].rearrange("p (e m j) -> p m j e", e=2, j=PACK),
-                in_=raw[:].rearrange("p j (m u e) -> p u m j e", u=2, e=2)[:, u],
+                out=grouped[:, :PAIR].rearrange("p (e m j) -> p m j e", e=2, j=PACK)[:, m],
+                in_=raw[:].rearrange("p j (m u e) -> p u m j e", u=2, e=2)[:, u, m],
             )
 
         def quantize(weights, u, grouped):
             codes, scales = weights
             pair = slice(2 * u * P, 2 * (u + 1) * P)
-            nc.vector.quantize_mx(out=codes[:, pair].bitcast(FP8X4), scales=scales[:, pair], in_=grouped[:])
+            nc.vector.quantize_mx(out=codes[:, pair].bitcast(FP8X4), scales=scales[:, pair], in_=grouped[:, :PAIR])
 
         def product(bank, weights, t, codes, scales, where):
             w_codes, w_scales = weights
@@ -68,10 +72,10 @@ def tile_picked_sharelay_none_p_kernel(tc, x_words, x_scales, w1, gn, w2, offs, 
         warm = sbuf("warm", [P, 1], F32)
         warm_out = sbuf("warm_out", [P, 1], F32)
         nc.vector.memset(warm[:], 0.0)
-        for q in range(4):
+        for r in range(4):
             nc.sync.dma_start(
-                out=x_scale_table[32 * q : 32 * q + 4, :].bitcast(I32),
-                in_=x_scales[0, 4 * q : 4 * q + 4, :].bitcast(I32),
+                out=x_scale_table[r:P:32, :].bitcast(I32),
+                in_=x_scales[0, r:16:4, :].bitcast(I32),
             )
         nc.scalar.activation(out=warm_out[:], in_=warm[:], func=ACT.Sigmoid, scale=-0.5)
 
@@ -110,9 +114,9 @@ def tile_picked_sharelay_none_p_kernel(tc, x_words, x_scales, w1, gn, w2, offs, 
         quantize(w1_mx, 1, w1_grouped[1])
 
         def products(stage, weights, codes, scales):
-            first = [psum.tile([P, HALF], F32, name="%s_half%d" % (stage, h), tag="half%d" % h) for h in range(2)]
-            for h in range(2):
-                product(first[h][:], weights, 0, codes, scales, cols[h])
+            first = [psum.tile([P, b - a], F32, name="%s_chunk%d" % (stage, c), tag="chunk%d" % c) for c, (a, b) in enumerate(CHUNKS)]
+            for c in range(len(CHUNKS)):
+                product(first[c][:], weights, 0, codes, scales, chunks[c])
             rest = {}
             for t in range(1, PACK):
                 rest[t] = psum.tile([P, S], F32, name="%s_bank%d" % (stage, t), tag="bank%d" % t)
@@ -129,28 +133,37 @@ def tile_picked_sharelay_none_p_kernel(tc, x_words, x_scales, w1, gn, w2, offs, 
         h_plain = [neg_win[t + 1][:, S:] for t in range(PACK - 1)] + [h_last[:]]
         diff = [sbuf("diff%d" % t, [P, S], F32) for t in range(PACK)]
         share = [sbuf("share%d" % t, [P, S], F32)[:] for t in range(PACK - 1)] + [neg_win[0][:, S:]]
-        z = [sbuf("z%d" % h, [P, PACK, HALF], F32) for h in range(2)]
+        z = [sbuf("z%d" % c, [P, PACK, b - a], F32) for c, (a, b) in enumerate(CHUNKS)]
 
-        def sigmoid(t, h):
-            nc.scalar.activation(out=share[t][:, cols[h]], in_=diff[t][:, cols[h]], func=ACT.Sigmoid, scale=slope[:, t : t + 1])
+        def sigmoid(t, c):
+            nc.scalar.activation(out=share[t][:, chunks[c]], in_=diff[t][:, chunks[c]], func=ACT.Sigmoid, scale=slope[:, t : t + 1])
 
-        def make_z(t, h):
-            nc.vector.tensor_tensor(z[h][:, t, :], y_win[t][:].indirect(n1_sb[:, entries[h]]), share[t][:, cols[h]], ALU.mult)
+        def make_z(t, c):
+            nc.vector.tensor_tensor(z[c][:, t, :], y_win[t][:].indirect(n1_sb[:, chunk_entries[c]]), share[t][:, chunks[c]], ALU.mult)
 
         def leave(dst, bank, t):
             nc.scalar.activation(out=dst, in_=bank, func=ACT.Copy, scale=gn_sb[:, t : t + 1])
 
         for t in range(PACK):
             if t == 0:
-                for h in range(2):
-                    leave(y_win[0][:, cols[h]], y_first[h][:], 0)
-                    leave(y_plain[0][:, cols[h]], y_first[h][:], 0)
+                leave(y_win[0][:, chunks[0]], y_first[0][:], 0)
+                leave(y_plain[0][:, chunks[0]], y_first[0][:], 0)
+                for c in range(1, len(CHUNKS)):
+                    leave(y_win[0][:, chunks[c]], y_first[c][:], 0)
+                for c in range(1, len(CHUNKS)):
+                    leave(y_plain[0][:, chunks[c]], y_first[c][:], 0)
                 for h in range(2):
                     nc.vector.tensor_tensor(diff[t][:, cols[h]], y_win[t][:].indirect(n2_sb[:, entries[h]]), y_plain[t][:, cols[h]], ALU.subtract)
             else:
                 leave(y_win[t][:, :S], y_rest[t][:], t)
-                leave(y_plain[t], y_rest[t][:], t)
-                nc.vector.tensor_tensor(diff[t][:], y_win[t][:].indirect(n2_sb[:]), y_plain[t], ALU.subtract)
+                if t == 1:
+                    for h in range(2):
+                        leave(y_plain[t][:, cols[h]], y_rest[t][:, cols[h]], t)
+                    for h in range(2):
+                        nc.vector.tensor_tensor(diff[t][:, cols[h]], y_win[t][:].indirect(n2_sb[:, entries[h]]), y_plain[t][:, cols[h]], ALU.subtract)
+                else:
+                    leave(y_plain[t], y_rest[t][:], t)
+                    nc.vector.tensor_tensor(diff[t][:], y_win[t][:].indirect(n2_sb[:]), y_plain[t], ALU.subtract)
                 sigmoid(t - 1, 0)
                 make_z(t - 1, 0)
         w2_grouped0 = sbuf("w2_grouped0", [P, 2 * P * PACK], BF16)
@@ -159,27 +172,25 @@ def tile_picked_sharelay_none_p_kernel(tc, x_words, x_scales, w1, gn, w2, offs, 
         quantize(w2_mx, 0, w2_grouped0)
         sigmoid(PACK - 1, 0)
         make_z(PACK - 1, 0)
-        for t in range(PACK):
-            sigmoid(t, 1)
-            make_z(t, 1)
+        for c in range(1, len(CHUNKS)):
+            for t in range(PACK):
+                sigmoid(t, c)
+                make_z(t, c)
 
-        z_grouped = [sbuf("z_grouped%d" % h, [P, HALF * PACK], BF16) for h in range(2)]
-
-        def weave(copy, h, c0, c1):
-            copy(
-                out=z_grouped[h][:, c0 * PACK : c1 * PACK].rearrange("p (c i t) -> p c t i", i=4, t=PACK),
-                in_=z[h][:, :, c0:c1].rearrange("p t (c i) -> p c t i", i=4),
-            )
-
-        weave(nc.scalar.copy, 0, 0, HALF)
-        weave(nc.vector.tensor_copy, 1, 0, VECTOR_COLS)
-        weave(nc.scalar.copy, 1, VECTOR_COLS, HALF)
+        w2_grouped1 = sbuf("w2_grouped1", [P, PAIR + PAIR // 4], BF16)
+        z_grouped = [sbuf("z_grouped%d" % c, [P, (b - a) * PACK], BF16)[:] for c, (a, b) in enumerate(CHUNKS[:-1])]
+        z_grouped.append(w2_grouped1[:, 3 * PAIR // 4 :])
         z_codes = sbuf("z_codes", [P, S], U32)
         z_scales = sbuf("z_scales", [P, S], U8)
-        for h in range(2):
-            nc.vector.quantize_mx(out=z_codes[:, cols[h]].bitcast(FP8X4), scales=z_scales[:, cols[h]], in_=z_grouped[h][:])
-        w2_grouped1 = sbuf("w2_grouped1", [P, 2 * P * PACK], BF16, tag="z_grouped1")
-        deal(nc.vector.tensor_copy, w2_raw, 1, w2_grouped1)
+        for c in range(len(CHUNKS)):
+            if c == len(CHUNKS) - 1:
+                deal(nc.scalar.copy, w2_raw, 1, w2_grouped1, slice(0, P // 2))
+            nc.scalar.copy(
+                out=z_grouped[c].rearrange("p (c i t) -> p c t i", i=4, t=PACK),
+                in_=z[c][:].rearrange("p t (c i) -> p c t i", i=4),
+            )
+            nc.vector.quantize_mx(out=z_codes[:, chunks[c]].bitcast(FP8X4), scales=z_scales[:, chunks[c]], in_=z_grouped[c])
+        deal(nc.vector.tensor_copy, w2_raw, 1, w2_grouped1, slice(P // 2, P))
         quantize(w2_mx, 1, w2_grouped1)
 
         h_first, h_rest = products("h", w2_mx, z_codes, z_scales)
@@ -195,10 +206,10 @@ def tile_picked_sharelay_none_p_kernel(tc, x_words, x_scales, w1, gn, w2, offs, 
 
         for t in range(PACK):
             if t == 0:
-                for h in range(2):
-                    nc.scalar.activation(out=neg_win[0][:, cols[h]], in_=h_first[h][:], func=ACT.Copy, scale=-1.0)
-                for h in range(2):
-                    nc.scalar.copy(out=h_plain[0][:, cols[h]], in_=h_first[h][:])
+                for c in range(len(CHUNKS)):
+                    nc.scalar.activation(out=neg_win[0][:, chunks[c]], in_=h_first[c][:], func=ACT.Copy, scale=-1.0)
+                for c in range(len(CHUNKS)):
+                    nc.scalar.copy(out=h_plain[0][:, chunks[c]], in_=h_first[c][:])
             else:
                 nc.scalar.activation(out=neg_win[t][:, :S], in_=h_rest[t][:], func=ACT.Copy, scale=-1.0)
                 nc.scalar.copy(out=h_plain[t], in_=h_rest[t][:])
@@ -210,5 +221,5 @@ def tile_picked_sharelay_none_p_kernel(tc, x_words, x_scales, w1, gn, w2, offs, 
             else:
                 for h in range(2):
                     nc.vector.tensor_tensor(gap[t][:, cols[h]], neg_win[t][:].indirect(n3_sb[:, entries[h]]), h_plain[t][:, cols[h]], ALU.add)
-        for h in range(2):
-            finish(PACK - 1, cols[h])
+        for c in range(len(CHUNKS)):
+            finish(PACK - 1, chunks[c])

@@ -1,6 +1,7 @@
 from contextlib import ExitStack
 
 import concourse.mybir as mybir
+from concourse.masks import make_identity
 
 K, T, S, N, H = 512, 2048, 512, 512, 512
 FLOPS = 2 * K * H * S + 2 * H * N * S
@@ -17,19 +18,19 @@ ACT = mybir.ActivationFunctionType
 
 P = 128
 PACK = 4
-HALF = S // 2
+GROUP = 16
 PAIR = 2 * P * PACK
-CHUNKS = ((0, 256), (256, 384), (384, 512))
-LARGEST = 2.0 ** 126
+LAST = PACK - 1
+ALL = slice(0, S)
+HALVES = (slice(0, S // 2), slice(S // 2, S))
+CHUNKS = (slice(0, 256), slice(256, 384), slice(384, 512))
+UNCUT_PLANE = 1
+TURNED = 2
+LARGEST = 2.0**126
 
 
 def tile_picked_sharelay_none_p_kernel(tc, x_words, x_scales, w1, gn, w2, offs, n1, n2, n3, n4, out):
     nc = tc.nc
-    cols = [slice(h * HALF, (h + 1) * HALF) for h in range(2)]
-    entries = [slice(h * HALF // 16, (h + 1) * HALF // 16) for h in range(2)]
-
-    chunks = [slice(a, b) for a, b in CHUNKS]
-    chunk_entries = [slice(a // 16, b // 16) for a, b in CHUNKS]
 
     with ExitStack() as ctx:
         keep = ctx.enter_context(tc.tile_pool(name="keep", bufs=1))
@@ -39,22 +40,25 @@ def tile_picked_sharelay_none_p_kernel(tc, x_words, x_scales, w1, gn, w2, offs, 
             return keep.tile(shape, dtype, name=name, tag=tag or name, align_bytes=64)
 
         def load_list(name, source):
-            tile = keep.tile([P, S // 16], U16, name=name)
+            tile = keep.tile([P, S // GROUP], U16, name=name)
             nc.sync.dma_start(tile[:], source)
             return tile
 
-        def load_weight(name, source):
-            tile = sbuf(name, [P, PACK, 512], F32, tag="raw_weight")
-            nc.sync.dma_start(out=tile[:], in_=source.rearrange("(p j) c -> p j c", j=PACK))
-            return tile
+        def look_up(window, lists, where):
+            return window[:].indirect(lists[:, where.start // GROUP : where.stop // GROUP])
 
-        def deal(copy, raw, u, grouped, m=slice(0, P)):
+        def load_weight(name, source):
+            raw = sbuf(name, [P, PACK, source.shape[1]], F32, tag="raw_weight")
+            nc.sync.dma_start(out=raw[:], in_=source.rearrange("(p j) c -> p j c", j=PACK))
+            return raw
+
+        def deal(copy, raw, u, grouped, m):
             copy(
                 out=grouped[:, :PAIR].rearrange("p (e m j) -> p m j e", e=2, j=PACK)[:, m],
                 in_=raw[:].rearrange("p j (m u e) -> p u m j e", u=2, e=2)[:, u, m],
             )
 
-        def quantize(weights, u, grouped):
+        def quantize_pair(weights, u, grouped):
             codes, scales = weights
             pair = slice(2 * u * P, 2 * (u + 1) * P)
             nc.vector.quantize_mx(out=codes[:, pair].bitcast(FP8X4), scales=scales[:, pair], in_=grouped[:, :PAIR])
@@ -63,21 +67,39 @@ def tile_picked_sharelay_none_p_kernel(tc, x_words, x_scales, w1, gn, w2, offs, 
             w_codes, w_scales = weights
             m = slice(t * P, (t + 1) * P)
             nc.tensor.matmul_mx(
-                out=bank, lhsT=w_codes[:, m].bitcast(FP8X4), lhsT_scale=w_scales[:, m],
-                rhs=codes[:, where].bitcast(FP8X4), rhs_scale=scales[:, where], start=True, stop=True,
+                out=bank[:],
+                lhsT=w_codes[:, m].bitcast(FP8X4),
+                lhsT_scale=w_scales[:, m],
+                rhs=codes[:, where].bitcast(FP8X4),
+                rhs_scale=scales[:, where],
+                start=True,
+                stop=True,
             )
+
+        def products(stage, weights, codes, scales):
+            chunk_banks = [
+                psum.tile([P, where.stop - where.start], F32, name="%s_chunk%d" % (stage, c), tag="chunk%d" % c)
+                for c, where in enumerate(CHUNKS)
+            ]
+            for bank, where in zip(chunk_banks, CHUNKS):
+                product(bank, weights, 0, codes, scales, where)
+            plane_banks = {}
+            for t in range(1, PACK):
+                plane_banks[t] = psum.tile([P, S], F32, name="%s_plane%d" % (stage, t), tag="plane%d" % t)
+                product(plane_banks[t], weights, t, codes, scales, ALL)
+            return chunk_banks, plane_banks
 
         x_scale_table = sbuf("x_scale_table", [P, T], U8)
         nc.vector.memset(x_scale_table[:].bitcast(I32), 0)
-        warm = sbuf("warm", [P, 1], F32)
-        warm_out = sbuf("warm_out", [P, 1], F32)
-        nc.vector.memset(warm[:], 0.0)
+        zero = sbuf("zero", [P, 1], F32)
+        one_half = sbuf("one_half", [P, 1], F32)
+        nc.vector.memset(zero[:], 0.0)
         for r in range(4):
             nc.sync.dma_start(
                 out=x_scale_table[r:P:32, :].bitcast(I32),
                 in_=x_scales[0, r:16:4, :].bitcast(I32),
             )
-        nc.scalar.activation(out=warm_out[:], in_=warm[:], func=ACT.Sigmoid, scale=-0.5)
+        nc.scalar.activation(out=one_half[:], in_=zero[:], func=ACT.Sigmoid)
 
         offs_sb = load_list("offs_sb", offs)
         w1_raw = load_weight("w1_raw", w1)
@@ -93,133 +115,149 @@ def tile_picked_sharelay_none_p_kernel(tc, x_words, x_scales, w1, gn, w2, offs, 
         n4_sb = load_list("n4_sb", n4)
         n3_sb = load_list("n3_sb", n3)
 
-        w1_grouped = [sbuf("w1_grouped%d" % u, [P, 2 * P * PACK], BF16) for u in range(2)]
-        deal(nc.vector.tensor_copy, w1_raw, 0, w1_grouped[0])
-        deal(nc.scalar.copy, w1_raw, 1, w1_grouped[1])
+        identity = sbuf("identity", [P, P], F32)
+        make_identity(nc, identity[:])
+
+        w1_grouped = [sbuf("w1_grouped%d" % u, [P, PAIR], BF16) for u in range(2)]
+        deal(nc.vector.tensor_copy, w1_raw, 0, w1_grouped[0], slice(0, P))
+        deal(nc.scalar.copy, w1_raw, 1, w1_grouped[1], slice(0, P))
         w2_raw = load_weight("w2_raw", w2)
+
         slope = sbuf("slope", [P, PACK], F32)
         bounded = sbuf("bounded", [P, PACK], F32)
         inverse = sbuf("inverse", [P, PACK], F32)
         nc.vector.reciprocal(inverse[:], gn_sb[:])
         nc.gpsimd.tensor_scalar(bounded[:], inverse[:], LARGEST, -LARGEST, ALU.min, ALU.max)
-        nc.gpsimd.tensor_scalar(slope[:], bounded[:], -0.5, 0.0, ALU.mult, ALU.add)
+        nc.gpsimd.tensor_scalar(slope[:], bounded[:], one_half[:], -1.0, ALU.mult, ALU.mult)
 
-        x_sc = sbuf("x_sc", [P, S], U8)
-        nc.vector.tensor_copy(x_sc[:], x_scale_table[:].indirect(offs_sb[:]))
+        picked_scales = sbuf("picked_scales", [P, S], U8)
+        nc.vector.tensor_copy(picked_scales[:], look_up(x_scale_table, offs_sb, ALL))
         w1_mx = sbuf("w1_codes", [P, H], U32, tag="x_scale_table"), sbuf("w1_scales", [P, H], U8)
-        quantize(w1_mx, 0, w1_grouped[0])
-        x_codes = sbuf("x_codes", [P, S], U32)
-        for h in range(2):
-            nc.vector.tensor_copy(x_codes[:, cols[h]], x_word_table[:].indirect(offs_sb[:, entries[h]]))
-        quantize(w1_mx, 1, w1_grouped[1])
+        quantize_pair(w1_mx, 0, w1_grouped[0])
+        picked_words = sbuf("picked_words", [P, S], U32)
+        for half in HALVES:
+            nc.vector.tensor_copy(picked_words[:, half], look_up(x_word_table, offs_sb, half))
+        quantize_pair(w1_mx, 1, w1_grouped[1])
 
-        def products(stage, weights, codes, scales):
-            first = [psum.tile([P, b - a], F32, name="%s_chunk%d" % (stage, c), tag="chunk%d" % c) for c, (a, b) in enumerate(CHUNKS)]
-            for c in range(len(CHUNKS)):
-                product(first[c][:], weights, 0, codes, scales, chunks[c])
-            rest = {}
-            for t in range(1, PACK):
-                rest[t] = psum.tile([P, S], F32, name="%s_bank%d" % (stage, t), tag="bank%d" % t)
-                product(rest[t][:], weights, t, codes, scales, slice(0, S))
-            return first, rest
+        y_chunks, y_planes = products("y", w1_mx, picked_words, picked_scales)
 
-        y_first, y_rest = products("y", w1_mx, x_codes, x_sc)
-
-        y_win = [sbuf("y_win%d" % t, [P, S if t == 0 else 2 * S], F32) for t in range(PACK)]
-        y_last = sbuf("y_last", [P, S], F32)
-        y_plain = [y_win[t + 1][:, S:] for t in range(PACK - 1)] + [y_last[:]]
-        neg_win = [sbuf("neg_win%d" % t, [P, 2 * S], F32) for t in range(PACK)]
+        g_window = [sbuf("g_window%d" % t, [P, S if t == 0 else 2 * S], F32) for t in range(PACK)]
+        g_last = sbuf("g_last", [P, S], F32)
+        g_plain = [g_window[t + 1][:, S:] for t in range(LAST)] + [g_last[:]]
+        neg_h_window = [sbuf("neg_h_window%d" % t, [P, 2 * S], F32) for t in range(PACK)]
         h_last = sbuf("h_last", [P, S], F32)
-        h_plain = [neg_win[t + 1][:, S:] for t in range(PACK - 1)] + [h_last[:]]
-        diff = [sbuf("diff%d" % t, [P, S], F32) for t in range(PACK)]
-        share = [sbuf("share%d" % t, [P, S], F32)[:] for t in range(PACK - 1)] + [neg_win[0][:, S:]]
-        z = [sbuf("z%d" % c, [P, PACK, b - a], F32) for c, (a, b) in enumerate(CHUNKS)]
+        h_plain = [neg_h_window[t + 1][:, S:] for t in range(LAST)] + [h_last[:]]
+        g_step = [sbuf("g_step%d" % t, [P, S], F32) for t in range(PACK)]
+        share = [sbuf("share%d" % t, [P, S], F32)[:] for t in range(LAST)] + [neg_h_window[0][:, S:]]
+        z = sbuf("z", [P, PACK, S], F32)
 
-        def sigmoid(t, c):
-            nc.scalar.activation(out=share[t][:, chunks[c]], in_=diff[t][:, chunks[c]], func=ACT.Sigmoid, scale=slope[:, t : t + 1])
-
-        def make_z(t, c):
-            nc.vector.tensor_tensor(z[c][:, t, :], y_win[t][:].indirect(n1_sb[:, chunk_entries[c]]), share[t][:, chunks[c]], ALU.mult)
-
-        def leave(dst, bank, t):
+        def scale_out(dst, bank, t):
             nc.scalar.activation(out=dst, in_=bank, func=ACT.Copy, scale=gn_sb[:, t : t + 1])
 
-        for t in range(PACK):
-            if t == 0:
-                leave(y_win[0][:, chunks[0]], y_first[0][:], 0)
-                leave(y_plain[0][:, chunks[0]], y_first[0][:], 0)
-                for c in range(1, len(CHUNKS)):
-                    leave(y_win[0][:, chunks[c]], y_first[c][:], 0)
-                for c in range(1, len(CHUNKS)):
-                    leave(y_plain[0][:, chunks[c]], y_first[c][:], 0)
-                for h in range(2):
-                    nc.vector.tensor_tensor(diff[t][:, cols[h]], y_win[t][:].indirect(n2_sb[:, entries[h]]), y_plain[t][:, cols[h]], ALU.subtract)
-            else:
-                leave(y_win[t][:, :S], y_rest[t][:], t)
-                if t == 1:
-                    for h in range(2):
-                        leave(y_plain[t][:, cols[h]], y_rest[t][:, cols[h]], t)
-                    for h in range(2):
-                        nc.vector.tensor_tensor(diff[t][:, cols[h]], y_win[t][:].indirect(n2_sb[:, entries[h]]), y_plain[t][:, cols[h]], ALU.subtract)
-                else:
-                    leave(y_plain[t], y_rest[t][:], t)
-                    nc.vector.tensor_tensor(diff[t][:], y_win[t][:].indirect(n2_sb[:]), y_plain[t], ALU.subtract)
-                sigmoid(t - 1, 0)
-                make_z(t - 1, 0)
-        w2_grouped0 = sbuf("w2_grouped0", [P, 2 * P * PACK], BF16)
-        deal(nc.scalar.copy, w2_raw, 0, w2_grouped0)
-        w2_mx = sbuf("w2_codes", [P, N], U32), sbuf("w2_scales", [P, N], U8)
-        quantize(w2_mx, 0, w2_grouped0)
-        sigmoid(PACK - 1, 0)
-        make_z(PACK - 1, 0)
-        for c in range(1, len(CHUNKS)):
-            for t in range(PACK):
-                sigmoid(t, c)
-                make_z(t, c)
+        def make_step(t, where):
+            nc.vector.tensor_tensor(g_step[t][:, where], look_up(g_window[t], n2_sb, where), g_plain[t][:, where], ALU.subtract)
 
+        def make_z(t, where):
+            nc.scalar.activation(out=share[t][:, where], in_=g_step[t][:, where], func=ACT.Sigmoid, scale=slope[:, t : t + 1])
+            nc.vector.tensor_tensor(z[:, t, where], look_up(g_window[t], n1_sb, where), share[t][:, where], ALU.mult)
+
+        scale_out(g_window[0][:, CHUNKS[0]], y_chunks[0][:], 0)
+        scale_out(g_plain[0][:, CHUNKS[0]], y_chunks[0][:], 0)
+        scale_out(g_window[0][:, CHUNKS[1]], y_chunks[1][:], 0)
+        nc.vector.tensor_scalar(g_window[0][:, CHUNKS[2]], y_chunks[2][:], gn_sb[:, 0:1], None, ALU.mult)
+        for bank, where in zip(y_chunks[1:], CHUNKS[1:]):
+            scale_out(g_plain[0][:, where], bank[:], 0)
+        for half in HALVES:
+            make_step(0, half)
+        for t in range(1, PACK):
+            pieces = HALVES if t == 1 else (ALL,)
+            scale_out(g_window[t][:, ALL], y_planes[t][:], t)
+            for where in pieces:
+                scale_out(g_plain[t][:, where], y_planes[t][:, where], t)
+            for where in pieces:
+                make_step(t, where)
+            make_z(t - 1, ALL if t - 1 == UNCUT_PLANE else CHUNKS[0])
+
+        w2_grouped0 = sbuf("w2_grouped0", [P, PAIR], BF16)
+        deal(nc.scalar.copy, w2_raw, 0, w2_grouped0, slice(0, P))
+        w2_mx = sbuf("w2_codes", [P, N], U32), sbuf("w2_scales", [P, N], U8)
+        quantize_pair(w2_mx, 0, w2_grouped0)
         w2_grouped1 = sbuf("w2_grouped1", [P, PAIR + PAIR // 4], BF16)
-        z_grouped = [sbuf("z_grouped%d" % c, [P, (b - a) * PACK], BF16)[:] for c, (a, b) in enumerate(CHUNKS[:-1])]
-        z_grouped.append(w2_grouped1[:, 3 * PAIR // 4 :])
+        deal(nc.scalar.copy, w2_raw, 1, w2_grouped1, slice(0, P // 2))
+
+        make_z(LAST, CHUNKS[0])
+        for where in CHUNKS[1:]:
+            for t in range(PACK):
+                if t != UNCUT_PLANE:
+                    make_z(t, where)
+
+        z_woven = [
+            sbuf("z_woven%d" % c, [P, (where.stop - where.start) * PACK], BF16)[:] for c, where in enumerate(CHUNKS[:-1])
+        ] + [w2_grouped1[:, 3 * PAIR // 4 :]]
         z_codes = sbuf("z_codes", [P, S], U32)
         z_scales = sbuf("z_scales", [P, S], U8)
-        for c in range(len(CHUNKS)):
-            if c == len(CHUNKS) - 1:
-                deal(nc.scalar.copy, w2_raw, 1, w2_grouped1, slice(0, P // 2))
+        for woven, where in zip(z_woven, CHUNKS):
             nc.scalar.copy(
-                out=z_grouped[c].rearrange("p (c i t) -> p c t i", i=4, t=PACK),
-                in_=z[c][:].rearrange("p t (c i) -> p c t i", i=4),
+                out=woven.rearrange("p (c i t) -> p c t i", i=4, t=PACK),
+                in_=z[:, :, where].rearrange("p t (c i) -> p c t i", i=4),
             )
-            nc.vector.quantize_mx(out=z_codes[:, chunks[c]].bitcast(FP8X4), scales=z_scales[:, chunks[c]], in_=z_grouped[c])
+            nc.vector.quantize_mx(out=z_codes[:, where].bitcast(FP8X4), scales=z_scales[:, where], in_=woven)
         deal(nc.vector.tensor_copy, w2_raw, 1, w2_grouped1, slice(P // 2, P))
-        quantize(w2_mx, 1, w2_grouped1)
+        quantize_pair(w2_mx, 1, w2_grouped1)
 
-        h_first, h_rest = products("h", w2_mx, z_codes, z_scales)
+        h_chunks, h_planes = products("h", w2_mx, z_codes, z_scales)
 
-        out_rows = out.rearrange("(p t) n -> p t n", t=PACK)
-        neg4 = [sbuf("neg4_%d" % t, [P, S], F32) for t in range(PACK)]
+        out_planes = out.rearrange("(p t) n -> p t n", t=PACK)
+        signed_half4 = [sbuf("signed_half4_%d" % t, [P, S], F32) for t in range(PACK)]
         gap = [sbuf("gap%d" % t, [P, S], F32) for t in range(PACK)]
         result = [sbuf("result%d" % t, [P, S], F32) for t in range(PACK)]
+        half4_turned = [sbuf("half4_turned%d" % t, [P, S], F32) for t in range(TURNED)]
+        excess_turned = [sbuf("excess_turned%d" % t, [P, S], F32) for t in range(TURNED)]
 
-        def finish(t, where):
-            nc.vector.tensor_tensor(result[t][:, where], neg4[t][:, where], gap[t][:, where], ALU.max)
-            nc.sync.dma_start(out=out_rows[:, t, where], in_=result[t][:, where])
+        def finish_on_vector(t, where):
+            nc.vector.tensor_tensor(result[t][:, where], signed_half4[t][:, where], gap[t][:, where], ALU.max)
+            nc.sync.dma_start(out=out_planes[:, t, where], in_=result[t][:, where])
+
+        def turned_sum(name, tag, terms):
+            bank = psum.tile([P, S], F32, name=name, tag=tag)
+            for b in range(S // P):
+                block = slice(b * P, (b + 1) * P)
+                for i, term in enumerate(terms):
+                    nc.tensor.matmul(
+                        bank[:, block],
+                        lhsT=term[:, block],
+                        rhs=identity[:],
+                        is_transpose=True,
+                        start=i == 0,
+                        stop=i == len(terms) - 1,
+                    )
+            return bank
 
         for t in range(PACK):
             if t == 0:
-                for c in range(len(CHUNKS)):
-                    nc.scalar.activation(out=neg_win[0][:, chunks[c]], in_=h_first[c][:], func=ACT.Copy, scale=-1.0)
-                for c in range(len(CHUNKS)):
-                    nc.scalar.copy(out=h_plain[0][:, chunks[c]], in_=h_first[c][:])
+                for bank, where in zip(h_chunks, CHUNKS):
+                    nc.scalar.activation(out=neg_h_window[0][:, where], in_=bank[:], func=ACT.Copy, scale=-1.0)
+                for bank, where in zip(h_chunks, CHUNKS):
+                    nc.scalar.copy(out=h_plain[0][:, where], in_=bank[:])
             else:
-                nc.scalar.activation(out=neg_win[t][:, :S], in_=h_rest[t][:], func=ACT.Copy, scale=-1.0)
-                nc.scalar.copy(out=h_plain[t], in_=h_rest[t][:])
-            nc.vector.tensor_scalar(neg4[t][:], neg_win[t][:].indirect(n4_sb[:]), -0.5, 0.0, ALU.mult, ALU.add)
-            if t > 0:
-                finish(t - 1, slice(0, S))
-            if t < PACK - 1:
-                nc.vector.tensor_tensor(gap[t][:], neg_win[t][:].indirect(n3_sb[:]), h_plain[t], ALU.add)
-            else:
-                for h in range(2):
-                    nc.vector.tensor_tensor(gap[t][:, cols[h]], neg_win[t][:].indirect(n3_sb[:, entries[h]]), h_plain[t][:, cols[h]], ALU.add)
-        for c in range(len(CHUNKS)):
-            finish(PACK - 1, chunks[c])
+                nc.scalar.activation(out=neg_h_window[t][:, ALL], in_=h_planes[t][:], func=ACT.Copy, scale=-1.0)
+                nc.scalar.copy(out=h_plain[t], in_=h_planes[t][:])
+            factor = 0.5 if t < TURNED else -0.5
+            nc.vector.tensor_scalar(signed_half4[t][:], look_up(neg_h_window[t], n4_sb, ALL), factor, 0.0, ALU.mult, ALU.add)
+            if t > TURNED:
+                finish_on_vector(t - 1, ALL)
+            for where in HALVES if t == LAST else (ALL,):
+                nc.vector.tensor_tensor(gap[t][:, where], look_up(neg_h_window[t], n3_sb, where), h_plain[t][:, where], ALU.add)
+
+        turn_banks = (("spare0", "spare1", "chunk0"), ("chunk1", "chunk2", "plane1"))
+        for t in range(TURNED):
+            bank = turned_sum("neg_half4_sum%d" % t, turn_banks[t][0], [signed_half4[t]])
+            nc.scalar.activation(out=half4_turned[t][:], in_=bank[:], func=ACT.Copy, scale=-1.0)
+            bank = turned_sum("excess_sum%d" % t, turn_banks[t][1], [gap[t], signed_half4[t]])
+            nc.scalar.activation(out=excess_turned[t][:], in_=bank[:], func=ACT.Relu)
+        for t in range(TURNED):
+            bank = turned_sum("result_sum%d" % t, turn_banks[t][2], [half4_turned[t], excess_turned[t]])
+            nc.scalar.copy(out=result[t][:], in_=bank[:])
+            nc.scalar.dma_start(out=out_planes[:, t, :], in_=result[t][:])
+        for where in CHUNKS:
+            finish_on_vector(LAST, where)

from contextlib import ExitStack

import concourse.mybir as mybir
from concourse.masks import make_identity

K, T, S, N, H = 512, 2048, 512, 512, 512
FLOPS = 2 * K * H * S + 2 * H * N * S

F32 = mybir.dt.float32
BF16 = mybir.dt.bfloat16
I32 = mybir.dt.int32
U32 = mybir.dt.uint32
U16 = mybir.dt.uint16
U8 = mybir.dt.uint8
FP8X4 = mybir.dt.float8_e4m3fn_x4
ALU = mybir.AluOpType
ACT = mybir.ActivationFunctionType

P = 128
PACK = 4
GROUP = 16
PAIR = 2 * P * PACK
LAST = PACK - 1
ALL = slice(0, S)
HALVES = (slice(0, S // 2), slice(S // 2, S))
CHUNKS = (slice(0, 256), slice(256, 384), slice(384, 512))
UNCUT_PLANE = 1
TURNED = 2
LARGEST = 2.0**126


def tile_picked_sharelay_none_p_kernel(tc, x_words, x_scales, w1, gn, w2, offs, n1, n2, n3, n4, out):
    nc = tc.nc

    with ExitStack() as ctx:
        keep = ctx.enter_context(tc.tile_pool(name="keep", bufs=1))
        psum = ctx.enter_context(tc.psum_pool(name="psum", bufs=1))

        def sbuf(name, shape, dtype, tag=None):
            return keep.tile(shape, dtype, name=name, tag=tag or name, align_bytes=64)

        def load_list(name, source):
            tile = keep.tile([P, S // GROUP], U16, name=name)
            nc.sync.dma_start(tile[:], source)
            return tile

        def look_up(window, lists, where):
            return window[:].indirect(lists[:, where.start // GROUP : where.stop // GROUP])

        def load_weight(name, source):
            raw = sbuf(name, [P, PACK, source.shape[1]], F32, tag="raw_weight")
            nc.sync.dma_start(out=raw[:], in_=source.rearrange("(p j) c -> p j c", j=PACK))
            return raw

        def deal(copy, raw, u, grouped, m):
            copy(
                out=grouped[:, :PAIR].rearrange("p (e m j) -> p m j e", e=2, j=PACK)[:, m],
                in_=raw[:].rearrange("p j (m u e) -> p u m j e", u=2, e=2)[:, u, m],
            )

        def quantize_pair(weights, u, grouped):
            codes, scales = weights
            pair = slice(2 * u * P, 2 * (u + 1) * P)
            nc.vector.quantize_mx(out=codes[:, pair].bitcast(FP8X4), scales=scales[:, pair], in_=grouped[:, :PAIR])

        def product(bank, weights, t, codes, scales, where):
            w_codes, w_scales = weights
            m = slice(t * P, (t + 1) * P)
            nc.tensor.matmul_mx(
                out=bank[:],
                lhsT=w_codes[:, m].bitcast(FP8X4),
                lhsT_scale=w_scales[:, m],
                rhs=codes[:, where].bitcast(FP8X4),
                rhs_scale=scales[:, where],
                start=True,
                stop=True,
            )

        def products(stage, weights, codes, scales):
            chunk_banks = [
                psum.tile([P, where.stop - where.start], F32, name="%s_chunk%d" % (stage, c), tag="chunk%d" % c)
                for c, where in enumerate(CHUNKS)
            ]
            for bank, where in zip(chunk_banks, CHUNKS):
                product(bank, weights, 0, codes, scales, where)
            plane_banks = {}
            for t in range(1, PACK):
                plane_banks[t] = psum.tile([P, S], F32, name="%s_plane%d" % (stage, t), tag="plane%d" % t)
                product(plane_banks[t], weights, t, codes, scales, ALL)
            return chunk_banks, plane_banks

        x_scale_table = sbuf("x_scale_table", [P, T], U8)
        nc.vector.memset(x_scale_table[:].bitcast(I32), 0)
        zero = sbuf("zero", [P, 1], F32)
        one_half = sbuf("one_half", [P, 1], F32)
        nc.vector.memset(zero[:], 0.0)
        for r in range(4):
            nc.sync.dma_start(
                out=x_scale_table[r:P:32, :].bitcast(I32),
                in_=x_scales[0, r:16:4, :].bitcast(I32),
            )
        nc.scalar.activation(out=one_half[:], in_=zero[:], func=ACT.Sigmoid)

        offs_sb = load_list("offs_sb", offs)
        w1_raw = load_weight("w1_raw", w1)
        gn_sb = sbuf("gn_sb", [P, PACK], F32)
        nc.sync.dma_start(out=gn_sb[:], in_=gn.rearrange("(p t) o -> p (t o)", t=PACK))
        n2_sb = load_list("n2_sb", n2)
        x_word_table = sbuf("x_word_table", [P, T], U32)
        nc.sync.dma_start(
            out=x_word_table[:].bitcast(I32),
            in_=x_words[0].rearrange("p n t -> p (n t)").bitcast(I32),
        )
        n1_sb = load_list("n1_sb", n1)
        n4_sb = load_list("n4_sb", n4)
        n3_sb = load_list("n3_sb", n3)

        identity = sbuf("identity", [P, P], F32)
        make_identity(nc, identity[:])

        w1_grouped = [sbuf("w1_grouped%d" % u, [P, PAIR], BF16) for u in range(2)]
        deal(nc.vector.tensor_copy, w1_raw, 0, w1_grouped[0], slice(0, P))
        deal(nc.scalar.copy, w1_raw, 1, w1_grouped[1], slice(0, P))
        w2_raw = load_weight("w2_raw", w2)

        slope = sbuf("slope", [P, PACK], F32)
        bounded = sbuf("bounded", [P, PACK], F32)
        inverse = sbuf("inverse", [P, PACK], F32)
        nc.vector.reciprocal(inverse[:], gn_sb[:])
        nc.gpsimd.tensor_scalar(bounded[:], inverse[:], LARGEST, -LARGEST, ALU.min, ALU.max)
        nc.gpsimd.tensor_scalar(slope[:], bounded[:], one_half[:], -1.0, ALU.mult, ALU.mult)

        picked_scales = sbuf("picked_scales", [P, S], U8)
        nc.vector.tensor_copy(picked_scales[:], look_up(x_scale_table, offs_sb, ALL))
        w1_mx = sbuf("w1_codes", [P, H], U32, tag="x_scale_table"), sbuf("w1_scales", [P, H], U8)
        quantize_pair(w1_mx, 0, w1_grouped[0])
        picked_words = sbuf("picked_words", [P, S], U32)
        for half in HALVES:
            nc.vector.tensor_copy(picked_words[:, half], look_up(x_word_table, offs_sb, half))
        quantize_pair(w1_mx, 1, w1_grouped[1])

        y_chunks, y_planes = products("y", w1_mx, picked_words, picked_scales)

        g_window = [sbuf("g_window%d" % t, [P, S if t == 0 else 2 * S], F32) for t in range(PACK)]
        g_last = sbuf("g_last", [P, S], F32)
        g_plain = [g_window[t + 1][:, S:] for t in range(LAST)] + [g_last[:]]
        neg_h_window = [sbuf("neg_h_window%d" % t, [P, 2 * S], F32) for t in range(PACK)]
        h_last = sbuf("h_last", [P, S], F32)
        h_plain = [neg_h_window[t + 1][:, S:] for t in range(LAST)] + [h_last[:]]
        g_step = [sbuf("g_step%d" % t, [P, S], F32) for t in range(PACK)]
        share = [sbuf("share%d" % t, [P, S], F32)[:] for t in range(LAST)] + [neg_h_window[0][:, S:]]
        z = sbuf("z", [P, PACK, S], F32)

        def scale_out(dst, bank, t):
            nc.scalar.activation(out=dst, in_=bank, func=ACT.Copy, scale=gn_sb[:, t : t + 1])

        def make_step(t, where):
            nc.vector.tensor_tensor(g_step[t][:, where], look_up(g_window[t], n2_sb, where), g_plain[t][:, where], ALU.subtract)

        def make_z(t, where):
            nc.scalar.activation(out=share[t][:, where], in_=g_step[t][:, where], func=ACT.Sigmoid, scale=slope[:, t : t + 1])
            nc.vector.tensor_tensor(z[:, t, where], look_up(g_window[t], n1_sb, where), share[t][:, where], ALU.mult)

        scale_out(g_window[0][:, CHUNKS[0]], y_chunks[0][:], 0)
        scale_out(g_plain[0][:, CHUNKS[0]], y_chunks[0][:], 0)
        scale_out(g_window[0][:, CHUNKS[1]], y_chunks[1][:], 0)
        nc.vector.tensor_scalar(g_window[0][:, CHUNKS[2]], y_chunks[2][:], gn_sb[:, 0:1], None, ALU.mult)
        for bank, where in zip(y_chunks[1:], CHUNKS[1:]):
            scale_out(g_plain[0][:, where], bank[:], 0)
        for half in HALVES:
            make_step(0, half)
        for t in range(1, PACK):
            pieces = HALVES if t == 1 else (ALL,)
            scale_out(g_window[t][:, ALL], y_planes[t][:], t)
            for where in pieces:
                scale_out(g_plain[t][:, where], y_planes[t][:, where], t)
            for where in pieces:
                make_step(t, where)
            make_z(t - 1, ALL if t - 1 == UNCUT_PLANE else CHUNKS[0])

        w2_grouped0 = sbuf("w2_grouped0", [P, PAIR], BF16)
        deal(nc.scalar.copy, w2_raw, 0, w2_grouped0, slice(0, P))
        w2_mx = sbuf("w2_codes", [P, N], U32), sbuf("w2_scales", [P, N], U8)
        quantize_pair(w2_mx, 0, w2_grouped0)
        w2_grouped1 = sbuf("w2_grouped1", [P, PAIR + PAIR // 4], BF16)
        deal(nc.scalar.copy, w2_raw, 1, w2_grouped1, slice(0, P // 2))

        make_z(LAST, CHUNKS[0])
        for where in CHUNKS[1:]:
            for t in range(PACK):
                if t != UNCUT_PLANE:
                    make_z(t, where)

        z_woven = [
            sbuf("z_woven%d" % c, [P, (where.stop - where.start) * PACK], BF16)[:] for c, where in enumerate(CHUNKS[:-1])
        ] + [w2_grouped1[:, 3 * PAIR // 4 :]]
        z_codes = sbuf("z_codes", [P, S], U32)
        z_scales = sbuf("z_scales", [P, S], U8)
        for woven, where in zip(z_woven, CHUNKS):
            nc.scalar.copy(
                out=woven.rearrange("p (c i t) -> p c t i", i=4, t=PACK),
                in_=z[:, :, where].rearrange("p t (c i) -> p c t i", i=4),
            )
            nc.vector.quantize_mx(out=z_codes[:, where].bitcast(FP8X4), scales=z_scales[:, where], in_=woven)
        deal(nc.vector.tensor_copy, w2_raw, 1, w2_grouped1, slice(P // 2, P))
        quantize_pair(w2_mx, 1, w2_grouped1)

        h_chunks, h_planes = products("h", w2_mx, z_codes, z_scales)

        out_planes = out.rearrange("(p t) n -> p t n", t=PACK)
        signed_half4 = [sbuf("signed_half4_%d" % t, [P, S], F32) for t in range(PACK)]
        gap = [sbuf("gap%d" % t, [P, S], F32) for t in range(PACK)]
        result = [sbuf("result%d" % t, [P, S], F32) for t in range(PACK)]
        half4_turned = [sbuf("half4_turned%d" % t, [P, S], F32) for t in range(TURNED)]
        excess_turned = [sbuf("excess_turned%d" % t, [P, S], F32) for t in range(TURNED)]

        def finish_on_vector(t, where):
            nc.vector.tensor_tensor(result[t][:, where], signed_half4[t][:, where], gap[t][:, where], ALU.max)
            nc.sync.dma_start(out=out_planes[:, t, where], in_=result[t][:, where])

        def turned_sum(name, tag, terms):
            bank = psum.tile([P, S], F32, name=name, tag=tag)
            for b in range(S // P):
                block = slice(b * P, (b + 1) * P)
                for i, term in enumerate(terms):
                    nc.tensor.matmul(
                        bank[:, block],
                        lhsT=term[:, block],
                        rhs=identity[:],
                        is_transpose=True,
                        start=i == 0,
                        stop=i == len(terms) - 1,
                    )
            return bank

        for t in range(PACK):
            if t == 0:
                for bank, where in zip(h_chunks, CHUNKS):
                    nc.scalar.activation(out=neg_h_window[0][:, where], in_=bank[:], func=ACT.Copy, scale=-1.0)
                for bank, where in zip(h_chunks, CHUNKS):
                    nc.scalar.copy(out=h_plain[0][:, where], in_=bank[:])
            else:
                nc.scalar.activation(out=neg_h_window[t][:, ALL], in_=h_planes[t][:], func=ACT.Copy, scale=-1.0)
                nc.scalar.copy(out=h_plain[t], in_=h_planes[t][:])
            factor = 0.5 if t < TURNED else -0.5
            nc.vector.tensor_scalar(signed_half4[t][:], look_up(neg_h_window[t], n4_sb, ALL), factor, 0.0, ALU.mult, ALU.add)
            if t > TURNED:
                finish_on_vector(t - 1, ALL)
            for where in HALVES if t == LAST else (ALL,):
                nc.vector.tensor_tensor(gap[t][:, where], look_up(neg_h_window[t], n3_sb, where), h_plain[t][:, where], ALU.add)

        turn_banks = (("spare0", "spare1", "chunk0"), ("chunk1", "chunk2", "plane1"))
        for t in range(TURNED):
            bank = turned_sum("neg_half4_sum%d" % t, turn_banks[t][0], [signed_half4[t]])
            nc.scalar.activation(out=half4_turned[t][:], in_=bank[:], func=ACT.Copy, scale=-1.0)
            bank = turned_sum("excess_sum%d" % t, turn_banks[t][1], [gap[t], signed_half4[t]])
            nc.scalar.activation(out=excess_turned[t][:], in_=bank[:], func=ACT.Relu)
        for t in range(TURNED):
            bank = turned_sum("result_sum%d" % t, turn_banks[t][2], [half4_turned[t], excess_turned[t]])
            nc.scalar.copy(out=result[t][:], in_=bank[:])
            nc.scalar.dma_start(out=out_planes[:, t, :], in_=result[t][:])
        for where in CHUNKS:
            finish_on_vector(LAST, where)
